import numpy as np
import ml_dtypes


def mxq(x, axis, fmt="e4m3"):
    dtype, down = {"e4m3": (ml_dtypes.float8_e4m3fn, 7), "e5m2": (ml_dtypes.float8_e5m2, 14)}[fmt]
    v = np.moveaxis(np.asarray(x, np.float32).astype(ml_dtypes.bfloat16).astype(np.float64), axis, -1)
    blocks = v.reshape(v.shape[:-1] + (-1, 32))
    amax = np.abs(blocks).max(-1, keepdims=True)
    byte = np.maximum(np.where(amax > 0, np.frexp(amax)[1] - 1 + 127, 0) - down, 1)
    scale = np.exp2(byte - 127.0)
    codes = (blocks / scale).astype(np.float32).astype(dtype).astype(np.float64)
    return np.moveaxis((codes * scale).reshape(v.shape), -1, axis)


WIDE = False


def mx_kscale(k, group=512):
    if not WIDE:
        return np.ones(k)
    levels = np.array([10, -10, 5, -5, 0])
    if group != 512:
        return np.exp2(np.random.permutation(np.resize(levels, k // group))).repeat(group)
    if k % 512:
        return np.exp2(np.random.permutation(np.resize(levels, k // 32))).repeat(32)
    a = np.empty((k // 512, 16))
    for p in range(k // 512):
        a[p, :8] = np.random.permutation(np.resize(levels, 8))
        for g in range(8):
            far = levels[np.abs(levels - a[p, g]) >= 10]
            a[p, g + 8] = far[np.random.randint(len(far))]
    return np.exp2(a.ravel()).repeat(32)


def f64(x):
    return np.asarray(x).astype(np.float64)


E2M1 = np.array([0.0, 0.5, 1.0, 1.5, 2.0, 3.0, 4.0, 6.0, -0.0, -0.5, -1.0, -1.5, -2.0, -3.0, -4.0, -6.0])


def pack_group(w):
    k, n = w.shape
    w = f64(np.asarray(w, np.float32).astype(ml_dtypes.bfloat16)).reshape(k // 32, 32, n)
    amax = np.abs(w).max(1)
    mant, ex = np.frexp(amax / 6.0)
    byte = np.clip(np.where(amax > 0, np.where(mant > 0.5, ex, ex - 1) + 127, 1), 1, 254)
    scaled = (w * np.exp2(127.0 - byte)[:, None, :]).reshape(k, n).astype(np.float32)
    c = np.ascontiguousarray(scaled.reshape(k // 4, 4, n).transpose(0, 2, 1)).astype(ml_dtypes.float4_e2m1fn).view(np.uint8) & 0xF
    return np.ascontiguousarray((c[..., 0::2] | (c[..., 1::2] << 4)).reshape(k // 4, 2 * n)), byte.astype(np.uint8)


def unpack_group(words, scales):
    p, n = words.shape[0], scales.shape[1]
    words = np.ascontiguousarray(words).reshape(p, n, 2)
    nib = np.empty((p, n, 4), np.uint8)
    nib[..., 0::2] = words & 0xF
    nib[..., 1::2] = words >> 4
    return E2M1[nib].transpose(0, 2, 1).reshape(4 * p, n) * np.repeat(np.exp2(scales.astype(np.float64) - 127.0), 32, axis=0)


G, D, M, N = 4, 256, 256, 512


def setup_inputs():
    n = np.random.standard_normal
    s = mx_kscale(D, 0)[:, None]
    w_ = [pack_group(w) for w in n((G, D, M)) / np.sqrt(D) / s]
    return {
        "x": (n((G, D, N)) * s).astype(np.float32),
        "w_words": np.stack([w[0] for w in w_]),
        "w_scales": np.stack([w[1] for w in w_]),
    }


def reference(x, w_words, w_scales):
    xq = mxq(f64(x), 1, "e4m3")
    y = np.stack([unpack_group(w_words[g], w_scales[g]) for g in range(G)]).transpose(0, 2, 1) @ xq
    y = np.maximum(y, 0.0)
    return y

@@ -1,0 +1,122 @@
+from contextlib import ExitStack
+
+import concourse.mybir as mybir
+
+G, D, M, N = 4, 256, 256, 512
+FLOPS = 2 * G * D * M * N
+
+F32 = mybir.dt.float32
+BF16 = mybir.dt.bfloat16
+I32 = mybir.dt.int32
+U32 = mybir.dt.uint32
+U8 = mybir.dt.uint8
+FP8X4 = mybir.dt.float8_e4m3fn_x4
+FP4X4 = mybir.dt.float4_e2m1fn_x4
+RELU = mybir.ActivationFunctionType.Relu
+
+P = 128
+PACK = 4
+ROWS = 64
+SETS = 2
+HALF = 256
+VEC_COLS = 168
+
+
+def tile_rows_glin_relu_kernel(tc, x, w_words, w_scales, out):
+    nc = tc.nc
+    x_v = x.rearrange("(s c) (p j) n -> s (c p) j n", c=2, j=PACK)
+    words_v = w_words.bitcast(I32).rearrange("(s c) p b -> (c p) s b", c=2)
+    scales_v = w_scales.bitcast(I32).rearrange("(s c) (h r) b -> r (c h) s b", c=2, r=4)
+    out_v = out.rearrange("(s c) (e p) n -> s e p c n", c=2, p=P)
+
+    with ExitStack() as ctx:
+        sb = ctx.enter_context(tc.tile_pool(name="sb", bufs=1))
+        ps = ctx.enter_context(tc.psum_pool(name="ps", bufs=1))
+        ctx.enter_context(tc.manual_schedule())
+
+        w_sb = sb.tile([P, SETS, 2 * M], U8, name="w_sb", align_bytes=64)
+        ws_sb = sb.tile([P, SETS, M], U8, name="ws_sb", align_bytes=64)
+        codes = sb.tile([P, SETS, N], U32, name="codes", align_bytes=64)
+        scales = sb.tile([P, SETS, N], U8, name="scales", align_bytes=64)
+        warm = sb.tile([P, 8], F32, name="warm")
+        raw = {}
+        grouped = {}
+        for s in range(SETS):
+            for h in range(2):
+                raw[s, h] = sb.tile([P, PACK, HALF], F32, name="raw%d%d" % (s, h), align_bytes=64)
+                grouped[s, h] = sb.tile([P, HALF, PACK], BF16, name="grouped%d%d" % (s, h), align_bytes=64)
+        acc = {}
+        res = {}
+        for s in range(SETS):
+            for e in range(2):
+                res[s, e] = sb.tile([P, 2, N], F32, name="res%d%d" % (s, e), align_bytes=64)
+                for c in range(2):
+                    acc[s, e, c] = ps.tile([P, N], F32, name="acc%d%d%d" % (s, e, c))
+
+        def load(s, h):
+            nc.sync.dma_start(out=raw[s, h][:], in_=x_v[s][:, :, h * HALF : (h + 1) * HALF])
+
+        nc.vector.memset(ws_sb[:].bitcast(I32), 0)
+        nc.vector.memset(warm[:], 0.0)
+        for r in range(4):
+            nc.scalar.dma_start(out=ws_sb[r:P:32, :, :].bitcast(I32), in_=scales_v[r])
+        nc.scalar.activation(out=warm[:, 4:5], in_=warm[:, 0:1], func=RELU)
+        load(0, 0)
+        load(0, 1)
+        nc.sync.dma_start(out=w_sb[:].bitcast(I32), in_=words_v)
+        load(1, 0)
+        load(1, 1)
+
+        def views(s, h, lo, hi):
+            dst = grouped[s, h][:, lo:hi, :].rearrange("p (a i) j -> p a j i", i=4)
+            src = raw[s, h][:, :, lo:hi].rearrange("p j (a i) -> p a j i", i=4)
+            return dst, src
+
+        def interleave(s, h):
+            dst, src = views(s, h, 0, VEC_COLS)
+            nc.vector.tensor_copy(out=dst, in_=src)
+            dst, src = views(s, h, VEC_COLS, HALF)
+            nc.scalar.copy(out=dst, in_=src)
+
+        def quantize(s, h):
+            cols = slice(h * HALF, (h + 1) * HALF)
+            nc.vector.quantize_mx(
+                out=codes[:, s, cols].bitcast(FP8X4),
+                scales=scales[:, s, cols],
+                in_=grouped[s, h][:].rearrange("p n j -> p (n j)"),
+            )
+
+        def multiply(s, e):
+            for c in range(2):
+                rows = slice(c * ROWS, (c + 1) * ROWS)
+                nc.tensor.matmul_mx(
+                    out=acc[s, e, c][:],
+                    lhsT=w_sb[rows, s, 2 * P * e : 2 * P * (e + 1)].bitcast(FP4X4),
+                    lhsT_scale=ws_sb[rows, s, P * e : P * (e + 1)],
+                    rhs=codes[rows, s, :].bitcast(FP8X4),
+                    rhs_scale=scales[rows, s, :],
+                    start=True,
+                    stop=True,
+                )
+
+        def finish(s, e):
+            nc.scalar.activation(out=res[s, e][:, 0, :], in_=acc[s, e, 0][:], func=RELU)
+            nc.vector.tensor_scalar_max(out=res[s, e][:, 1, :], in0=acc[s, e, 1][:], scalar1=0.0)
+            nc.sync.dma_start(out=out_v[s, e], in_=res[s, e][:])
+
+        interleave(0, 0)
+        quantize(0, 0)
+        interleave(0, 1)
+        quantize(0, 1)
+        multiply(0, 0)
+        multiply(0, 1)
+        interleave(1, 0)
+        finish(0, 0)
+        quantize(1, 0)
+        interleave(1, 1)
+        quantize(1, 1)
+        finish(0, 1)
+        multiply(1, 0)
+        multiply(1, 1)
+        finish(1, 0)
+        finish(1, 1)

@@ -19,15 +19,16 @@ PACK = 4
 ROWS = 64
 SETS = 2
 HALF = 256
+STAGES = 4
 VEC_COLS = 168
 
 
 def tile_rows_glin_relu_kernel(tc, x, w_words, w_scales, out):
     nc = tc.nc
-    x_v = x.rearrange("(s c) (p j) n -> s (c p) j n", c=2, j=PACK)
+    x_v = x.rearrange("(s c) (p j) (h n) -> s h (c p) j n", c=2, j=PACK, h=2)
     words_v = w_words.bitcast(I32).rearrange("(s c) p b -> (c p) s b", c=2)
-    scales_v = w_scales.bitcast(I32).rearrange("(s c) (h r) b -> r (c h) s b", c=2, r=4)
-    out_v = out.rearrange("(s c) (e p) n -> s e p c n", c=2, p=P)
+    scales_v = w_scales.bitcast(I32).rearrange("(s c) (q r) b -> r (c q) s b", c=2, r=4)
+    out_v = out.rearrange("(s c) (e p) (h n) -> s h e p c n", c=2, p=P, h=2)
 
     with ExitStack() as ctx:
         sb = ctx.enter_context(tc.tile_pool(name="sb", bufs=1))
@@ -36,87 +37,82 @@ def tile_rows_glin_relu_kernel(tc, x, w_words, w_scales, out):
 
         w_sb = sb.tile([P, SETS, 2 * M], U8, name="w_sb", align_bytes=64)
         ws_sb = sb.tile([P, SETS, M], U8, name="ws_sb", align_bytes=64)
-        codes = sb.tile([P, SETS, N], U32, name="codes", align_bytes=64)
-        scales = sb.tile([P, SETS, N], U8, name="scales", align_bytes=64)
+        codes = sb.tile([P, (STAGES + 1) * HALF], U32, name="codes", align_bytes=64)
+        scales = sb.tile([P, (STAGES + 1) * HALF], U8, name="scales", align_bytes=64)
         warm = sb.tile([P, 8], F32, name="warm")
-        raw = {}
-        grouped = {}
-        for s in range(SETS):
-            for h in range(2):
-                raw[s, h] = sb.tile([P, PACK, HALF], F32, name="raw%d%d" % (s, h), align_bytes=64)
-                grouped[s, h] = sb.tile([P, HALF, PACK], BF16, name="grouped%d%d" % (s, h), align_bytes=64)
-        acc = {}
+        raw = [sb.tile([P, PACK, HALF], F32, name="raw%d" % k, align_bytes=64) for k in range(STAGES)]
+        grouped = [sb.tile([P, HALF, PACK], BF16, name="grouped%d" % k, align_bytes=64) for k in range(STAGES)]
         res = {}
-        for s in range(SETS):
-            for e in range(2):
-                res[s, e] = sb.tile([P, 2, N], F32, name="res%d%d" % (s, e), align_bytes=64)
-                for c in range(2):
-                    acc[s, e, c] = ps.tile([P, N], F32, name="acc%d%d%d" % (s, e, c))
+        acc = {}
+        for e in range(2):
+            for k in range(STAGES):
+                res[k, e] = sb.tile([P, 2, HALF], F32, name="res%d%d" % (k, e), align_bytes=64)
+            for c in range(2):
+                for b in range(2):
+                    acc[b, e, c] = ps.tile([P, N], F32, name="acc%d%d%d" % (b, e, c))
 
-        def load(s, h):
-            nc.sync.dma_start(out=raw[s, h][:], in_=x_v[s][:, :, h * HALF : (h + 1) * HALF])
+        def load(k):
+            nc.sync.dma_start(out=raw[k][:], in_=x_v[k // 2, k % 2])
 
         nc.vector.memset(ws_sb[:].bitcast(I32), 0)
         nc.vector.memset(warm[:], 0.0)
+        nc.vector.memset(codes[:, 0:HALF], 0)
+        nc.vector.memset(scales[:, 0:HALF].bitcast(I32), 0)
         for r in range(4):
             nc.scalar.dma_start(out=ws_sb[r:P:32, :, :].bitcast(I32), in_=scales_v[r])
         nc.scalar.activation(out=warm[:, 4:5], in_=warm[:, 0:1], func=RELU)
-        load(0, 0)
-        load(0, 1)
+        load(0)
         nc.sync.dma_start(out=w_sb[:].bitcast(I32), in_=words_v)
-        load(1, 0)
-        load(1, 1)
+        for k in range(1, STAGES):
+            load(k)
 
-        def views(s, h, lo, hi):
-            dst = grouped[s, h][:, lo:hi, :].rearrange("p (a i) j -> p a j i", i=4)
-            src = raw[s, h][:, :, lo:hi].rearrange("p j (a i) -> p a j i", i=4)
+        def views(k, lo, hi):
+            dst = grouped[k][:, lo:hi, :].rearrange("p (a i) j -> p a j i", i=4)
+            src = raw[k][:, :, lo:hi].rearrange("p j (a i) -> p a j i", i=4)
             return dst, src
 
-        def interleave(s, h):
-            dst, src = views(s, h, 0, VEC_COLS)
+        def interleave(k):
+            dst, src = views(k, 0, VEC_COLS)
             nc.vector.tensor_copy(out=dst, in_=src)
-            dst, src = views(s, h, VEC_COLS, HALF)
+            dst, src = views(k, VEC_COLS, HALF)
             nc.scalar.copy(out=dst, in_=src)
 
-        def quantize(s, h):
-            cols = slice(h * HALF, (h + 1) * HALF)
+        def quantize(k):
+            cols = slice((k + 1) * HALF, (k + 2) * HALF)
             nc.vector.quantize_mx(
-                out=codes[:, s, cols].bitcast(FP8X4),
-                scales=scales[:, s, cols],
-                in_=grouped[s, h][:].rearrange("p n j -> p (n j)"),
+                out=codes[:, cols].bitcast(FP8X4),
+                scales=scales[:, cols],
+                in_=grouped[k][:].rearrange("p n j -> p (n j)"),
             )
 
-        def multiply(s, e):
+        def multiply(k, e):
+            s = k // 2
+            window = slice(k * HALF, k * HALF + N)
             for c in range(2):
                 rows = slice(c * ROWS, (c + 1) * ROWS)
                 nc.tensor.matmul_mx(
-                    out=acc[s, e, c][:],
+                    out=acc[k % 2, e, c][:],
                     lhsT=w_sb[rows, s, 2 * P * e : 2 * P * (e + 1)].bitcast(FP4X4),
                     lhsT_scale=ws_sb[rows, s, P * e : P * (e + 1)],
-                    rhs=codes[rows, s, :].bitcast(FP8X4),
-                    rhs_scale=scales[rows, s, :],
+                    rhs=codes[rows, window].bitcast(FP8X4),
+                    rhs_scale=scales[rows, window],
                     start=True,
                     stop=True,
                 )
 
-        def finish(s, e):
-            nc.scalar.activation(out=res[s, e][:, 0, :], in_=acc[s, e, 0][:], func=RELU)
-            nc.vector.tensor_scalar_max(out=res[s, e][:, 1, :], in0=acc[s, e, 1][:], scalar1=0.0)
-            nc.sync.dma_start(out=out_v[s, e], in_=res[s, e][:])
+        def finish(k, e):
+            nc.scalar.activation(out=res[k, e][:, 0, :], in_=acc[k % 2, e, 0][:, HALF:N], func=RELU)
+            nc.vector.tensor_scalar_max(out=res[k, e][:, 1, :], in0=acc[k % 2, e, 1][:, HALF:N], scalar1=0.0)
+            nc.sync.dma_start(out=out_v[k // 2, k % 2, e], in_=res[k, e][:])
 
-        interleave(0, 0)
-        quantize(0, 0)
-        interleave(0, 1)
-        quantize(0, 1)
-        multiply(0, 0)
-        multiply(0, 1)
-        interleave(1, 0)
-        finish(0, 0)
-        quantize(1, 0)
-        interleave(1, 1)
-        quantize(1, 1)
-        finish(0, 1)
-        multiply(1, 0)
-        multiply(1, 1)
-        finish(1, 0)
-        finish(1, 1)
+        for k in range(STAGES + 2):
+            if k < STAGES:
+                interleave(k)
+            if k >= 2:
+                finish(k - 2, 1)
+            if k < STAGES:
+                quantize(k)
+                multiply(k, 0)
+                multiply(k, 1)
+            if 1 <= k <= STAGES:
+                finish(k - 1, 0)

@@ -58,10 +58,10 @@ def tile_rows_glin_relu_kernel(tc, x, w_words, w_scales, out):
         nc.vector.memset(warm[:], 0.0)
         nc.vector.memset(codes[:, 0:HALF], 0)
         nc.vector.memset(scales[:, 0:HALF].bitcast(I32), 0)
-        for r in range(4):
-            nc.scalar.dma_start(out=ws_sb[r:P:32, :, :].bitcast(I32), in_=scales_v[r])
         nc.scalar.activation(out=warm[:, 4:5], in_=warm[:, 0:1], func=RELU)
         load(0)
+        for r in range(4):
+            nc.sync.dma_start(out=ws_sb[r:P:32, :, :].bitcast(I32), in_=scales_v[r])
         nc.sync.dma_start(out=w_sb[:].bitcast(I32), in_=words_v)
         for k in range(1, STAGES):
             load(k)

@@ -20,7 +20,8 @@ ROWS = 64
 SETS = 2
 HALF = 256
 STAGES = 4
-VEC_COLS = 168
+PIECE = 128
+VEC_COLS = 192
 
 
 def tile_rows_glin_relu_kernel(tc, x, w_words, w_scales, out):
@@ -62,9 +63,10 @@ def tile_rows_glin_relu_kernel(tc, x, w_words, w_scales, out):
         load(0)
         for r in range(4):
             nc.sync.dma_start(out=ws_sb[r:P:32, :, :].bitcast(I32), in_=scales_v[r])
-        nc.sync.dma_start(out=w_sb[:].bitcast(I32), in_=words_v)
+        nc.sync.dma_start(out=w_sb[:, 0, :].bitcast(I32), in_=words_v[:, 0, :])
         for k in range(1, STAGES):
             load(k)
+        nc.sync.dma_start(out=w_sb[:, 1, :].bitcast(I32), in_=words_v[:, 1, :])
 
         def views(k, lo, hi):
             dst = grouped[k][:, lo:hi, :].rearrange("p (a i) j -> p a j i", i=4)
@@ -72,18 +74,20 @@ def tile_rows_glin_relu_kernel(tc, x, w_words, w_scales, out):
             return dst, src
 
         def interleave(k):
-            dst, src = views(k, 0, VEC_COLS)
-            nc.vector.tensor_copy(out=dst, in_=src)
+            for lo, hi in ((0, PIECE), (PIECE, VEC_COLS)):
+                dst, src = views(k, lo, hi)
+                nc.vector.tensor_copy(out=dst, in_=src)
             dst, src = views(k, VEC_COLS, HALF)
             nc.scalar.copy(out=dst, in_=src)
 
         def quantize(k):
-            cols = slice((k + 1) * HALF, (k + 2) * HALF)
-            nc.vector.quantize_mx(
-                out=codes[:, cols].bitcast(FP8X4),
-                scales=scales[:, cols],
-                in_=grouped[k][:].rearrange("p n j -> p (n j)"),
-            )
+            for lo in range(0, HALF, PIECE):
+                cols = slice((k + 1) * HALF + lo, (k + 1) * HALF + lo + PIECE)
+                nc.vector.quantize_mx(
+                    out=codes[:, cols].bitcast(FP8X4),
+                    scales=scales[:, cols],
+                    in_=grouped[k][:, lo : lo + PIECE, :].rearrange("p n j -> p (n j)"),
+                )
 
         def multiply(k, e):
             s = k // 2
@@ -105,14 +109,20 @@ def tile_rows_glin_relu_kernel(tc, x, w_words, w_scales, out):
             nc.vector.tensor_scalar_max(out=res[k, e][:, 1, :], in0=acc[k % 2, e, 1][:, HALF:N], scalar1=0.0)
             nc.sync.dma_start(out=out_v[k // 2, k % 2, e], in_=res[k, e][:])
 
-        for k in range(STAGES + 2):
-            if k < STAGES:
-                interleave(k)
+        def finish_on_scalar(k, e):
+            for c in range(2):
+                nc.scalar.activation(out=res[k, e][:, c, :], in_=acc[k % 2, e, c][:, HALF:N], func=RELU)
+                nc.sync.dma_start(out=out_v[k // 2, k % 2, e][:, c, :], in_=res[k, e][:, c, :])
+
+        for k in range(STAGES):
+            interleave(k)
             if k >= 2:
-                finish(k - 2, 1)
-            if k < STAGES:
-                quantize(k)
-                multiply(k, 0)
-                multiply(k, 1)
-            if 1 <= k <= STAGES:
+                finish_on_scalar(k - 2, 1)
+            quantize(k)
+            multiply(k, 0)
+            multiply(k, 1)
+            if k >= 1:
                 finish(k - 1, 0)
+        finish(STAGES - 2, 1)
+        finish(STAGES - 1, 0)
+        finish(STAGES - 1, 1)

@@ -21,7 +21,7 @@ SETS = 2
 HALF = 256
 STAGES = 4
 PIECE = 128
-VEC_COLS = 192
+VEC_COLS = (160, 160, 192, 192)
 
 
 def tile_rows_glin_relu_kernel(tc, x, w_words, w_scales, out):
@@ -74,10 +74,10 @@ def tile_rows_glin_relu_kernel(tc, x, w_words, w_scales, out):
             return dst, src
 
         def interleave(k):
-            for lo, hi in ((0, PIECE), (PIECE, VEC_COLS)):
+            for lo, hi in ((0, PIECE), (PIECE, VEC_COLS[k])):
                 dst, src = views(k, lo, hi)
                 nc.vector.tensor_copy(out=dst, in_=src)
-            dst, src = views(k, VEC_COLS, HALF)
+            dst, src = views(k, VEC_COLS[k], HALF)
             nc.scalar.copy(out=dst, in_=src)
 
         def quantize(k):
@@ -116,12 +116,14 @@ def tile_rows_glin_relu_kernel(tc, x, w_words, w_scales, out):
 
         for k in range(STAGES):
             interleave(k)
+            if k == 1:
+                finish_on_scalar(0, 0)
             if k >= 2:
                 finish_on_scalar(k - 2, 1)
             quantize(k)
             multiply(k, 0)
             multiply(k, 1)
-            if k >= 1:
+            if k >= 2:
                 finish(k - 1, 0)
         finish(STAGES - 2, 1)
         finish(STAGES - 1, 0)

@@ -36,18 +36,17 @@ def tile_rows_glin_relu_kernel(tc, x, w_words, w_scales, out):
         ps = ctx.enter_context(tc.psum_pool(name="ps", bufs=1))
         ctx.enter_context(tc.manual_schedule())
 
-        w_sb = sb.tile([P, SETS, 2 * M], U8, name="w_sb", align_bytes=64)
-        ws_sb = sb.tile([P, SETS, M], U8, name="ws_sb", align_bytes=64)
-        codes = sb.tile([P, (STAGES + 1) * HALF], U32, name="codes", align_bytes=64)
-        scales = sb.tile([P, (STAGES + 1) * HALF], U8, name="scales", align_bytes=64)
-        warm = sb.tile([P, 8], F32, name="warm")
-        raw = [sb.tile([P, PACK, HALF], F32, name="raw%d" % k, align_bytes=64) for k in range(STAGES)]
-        grouped = [sb.tile([P, HALF, PACK], BF16, name="grouped%d" % k, align_bytes=64) for k in range(STAGES)]
+        w_sb = sb.tile([P, SETS, 2 * M], U8, name="w_sb", align_bytes=256)
+        ws_sb = sb.tile([P, SETS, M], U8, name="ws_sb", align_bytes=256)
+        codes = sb.tile([P, (STAGES + 1) * HALF], U32, name="codes", align_bytes=256)
+        scales = sb.tile([P, (STAGES + 1) * HALF], U8, name="scales", align_bytes=256)
+        raw = [sb.tile([P, PACK, HALF], F32, name="raw%d" % k, align_bytes=256) for k in range(STAGES)]
+        grouped = [sb.tile([P, HALF, PACK], BF16, name="grouped%d" % k, align_bytes=256) for k in range(STAGES)]
         res = {}
         acc = {}
         for e in range(2):
             for k in range(STAGES):
-                res[k, e] = sb.tile([P, 2, HALF], F32, name="res%d%d" % (k, e), align_bytes=64)
+                res[k, e] = sb.tile([P, 2, HALF], F32, name="res%d%d" % (k, e), align_bytes=256)
             for c in range(2):
                 for b in range(2):
                     acc[b, e, c] = ps.tile([P, N], F32, name="acc%d%d%d" % (b, e, c))
@@ -56,10 +55,8 @@ def tile_rows_glin_relu_kernel(tc, x, w_words, w_scales, out):
             nc.sync.dma_start(out=raw[k][:], in_=x_v[k // 2, k % 2])
 
         nc.vector.memset(ws_sb[:].bitcast(I32), 0)
-        nc.vector.memset(warm[:], 0.0)
         nc.vector.memset(codes[:, 0:HALF], 0)
         nc.vector.memset(scales[:, 0:HALF].bitcast(I32), 0)
-        nc.scalar.activation(out=warm[:, 4:5], in_=warm[:, 0:1], func=RELU)
         load(0)
         for r in range(4):
             nc.sync.dma_start(out=ws_sb[r:P:32, :, :].bitcast(I32), in_=scales_v[r])

@@ -21,107 +21,169 @@ SETS = 2
 HALF = 256
 STAGES = 4
 PIECE = 128
-VEC_COLS = (160, 160, 192, 192)
-
+ALIGN = 256
+PAD = 256
 
 def tile_rows_glin_relu_kernel(tc, x, w_words, w_scales, out):
     nc = tc.nc
-    x_v = x.rearrange("(s c) (p j) (h n) -> s h (c p) j n", c=2, j=PACK, h=2)
+    x_v = x.rearrange("(s c) (p j) n -> s (c p) j n", c=2, j=PACK)
     words_v = w_words.bitcast(I32).rearrange("(s c) p b -> (c p) s b", c=2)
     scales_v = w_scales.bitcast(I32).rearrange("(s c) (q r) b -> r (c q) s b", c=2, r=4)
-    out_v = out.rearrange("(s c) (e p) (h n) -> s h e p c n", c=2, p=P, h=2)
+    out_v = out.rearrange("(s c) (e p) n -> s p c e n", c=2, p=P)
 
     with ExitStack() as ctx:
         sb = ctx.enter_context(tc.tile_pool(name="sb", bufs=1))
         ps = ctx.enter_context(tc.psum_pool(name="ps", bufs=1))
         ctx.enter_context(tc.manual_schedule())
 
-        w_sb = sb.tile([P, SETS, 2 * M], U8, name="w_sb", align_bytes=256)
-        ws_sb = sb.tile([P, SETS, M], U8, name="ws_sb", align_bytes=256)
-        codes = sb.tile([P, (STAGES + 1) * HALF], U32, name="codes", align_bytes=256)
-        scales = sb.tile([P, (STAGES + 1) * HALF], U8, name="scales", align_bytes=256)
-        raw = [sb.tile([P, PACK, HALF], F32, name="raw%d" % k, align_bytes=256) for k in range(STAGES)]
-        grouped = [sb.tile([P, HALF, PACK], BF16, name="grouped%d" % k, align_bytes=256) for k in range(STAGES)]
-        res = {}
+        w_sb = sb.tile([P, SETS, 2 * M], U8, name="w_sb", align_bytes=ALIGN)
+        ws_sb = sb.tile([P, SETS, M], U8, name="ws_sb", align_bytes=ALIGN)
+        codes = sb.tile([P, PAD + SETS * N], U32, name="codes", align_bytes=ALIGN)
+        scales = sb.tile([P, PAD + SETS * N], U8, name="scales", align_bytes=ALIGN)
         acc = {}
-        for e in range(2):
-            for k in range(STAGES):
-                res[k, e] = sb.tile([P, 2, HALF], F32, name="res%d%d" % (k, e), align_bytes=256)
-            for c in range(2):
-                for b in range(2):
+        for b in range(2):
+            for e in range(2):
+                for c in range(2):
                     acc[b, e, c] = ps.tile([P, N], F32, name="acc%d%d%d" % (b, e, c))
+        raw = {}
+        grouped = {}
+        res = {}
+        ends = {}
 
-        def load(k):
-            nc.sync.dma_start(out=raw[k][:], in_=x_v[k // 2, k % 2])
+        def find(tiles, s, lo):
+            base = max(b for (ss, b) in tiles if ss == s and b <= lo)
+            return tiles[s, base], base
+
+        def load(s, lo, hi):
+            raw[s, lo] = sb.tile([P, PACK, hi - lo], F32, name="raw%d_%d" % (s, lo), align_bytes=ALIGN)
+            grouped[s, lo] = sb.tile([P, hi - lo, PACK], BF16, name="grouped%d_%d" % (s, lo), align_bytes=ALIGN)
+            nc.sync.dma_start(out=raw[s, lo][:], in_=x_v[s][:, :, lo:hi])
+
+        def result(s, lo, hi):
+            res[s, lo] = sb.tile([P, 2, 2, hi - lo], F32, name="res%d_%d" % (s, lo), align_bytes=ALIGN)
+
+        def load_scales():
+            for r in range(4):
+                nc.sync.dma_start(out=ws_sb[r:P:32, :, :].bitcast(I32), in_=scales_v[r])
+
+        def load_words(lo, hi):
+            nc.sync.dma_start(out=w_sb[:, lo:hi, :].bitcast(I32), in_=words_v[:, lo:hi, :])
+
+        def interleave(on_vector, s, lo, hi):
+            t, base = find(raw, s, lo)
+            dst = grouped[s, base][:, lo - base : hi - base, :].rearrange("p (a i) j -> p a j i", i=4)
+            src = t[:, :, lo - base : hi - base].rearrange("p j (a i) -> p a j i", i=4)
+            if on_vector:
+                nc.vector.tensor_copy(out=dst, in_=src)
+            else:
+                nc.scalar.copy(out=dst, in_=src)
+
+        def quantize(s, lo, hi):
+            t, base = find(grouped, s, lo)
+            cols = slice(PAD + s * N + lo, PAD + s * N + hi)
+            nc.vector.quantize_mx(
+                out=codes[:, cols].bitcast(FP8X4),
+                scales=scales[:, cols],
+                in_=t[:, lo - base : hi - base, :].rearrange("p n j -> p (n j)"),
+            )
+
+        def multiply(b, s, hi, halves):
+            window = slice(PAD + s * N + hi - N, PAD + s * N + hi)
+            for e in halves:
+                ends[b, e] = hi
+                for c in range(2):
+                    rows = slice(c * ROWS, (c + 1) * ROWS)
+                    nc.tensor.matmul_mx(
+                        out=acc[b, e, c][:],
+                        lhsT=w_sb[rows, s, 2 * P * e : 2 * P * (e + 1)].bitcast(FP4X4),
+                        lhsT_scale=ws_sb[rows, s, P * e : P * (e + 1)],
+                        rhs=codes[rows, window].bitcast(FP8X4),
+                        rhs_scale=scales[rows, window],
+                        start=True,
+                        stop=True,
+                    )
+
+        def relu(on_vector, b, e, c, s, lo, hi):
+            t, base = find(res, s, lo)
+            dst = t[:, c, e, lo - base : hi - base]
+            src = acc[b, e, c][:, N - ends[b, e] + lo : N - ends[b, e] + hi]
+            if on_vector:
+                nc.vector.tensor_scalar_max(out=dst, in0=src, scalar1=0.0)
+            else:
+                nc.scalar.activation(out=dst, in_=src, func=RELU)
+
+        def store(s, lo, e, c):
+            t = res[s, lo]
+            hi = lo + t.shape[3]
+            if e is None:
+                nc.sync.dma_start(out=out_v[s][:, :, :, lo:hi], in_=t[:])
+            elif c is None:
+                nc.sync.dma_start(out=out_v[s][:, :, e, lo:hi], in_=t[:, :, e, :])
+            else:
+                nc.sync.dma_start(out=out_v[s][:, c, e, lo:hi], in_=t[:, c, e, :])
 
         nc.vector.memset(ws_sb[:].bitcast(I32), 0)
-        nc.vector.memset(codes[:, 0:HALF], 0)
-        nc.vector.memset(scales[:, 0:HALF].bitcast(I32), 0)
-        load(0)
-        for r in range(4):
-            nc.sync.dma_start(out=ws_sb[r:P:32, :, :].bitcast(I32), in_=scales_v[r])
-        nc.sync.dma_start(out=w_sb[:, 0, :].bitcast(I32), in_=words_v[:, 0, :])
-        for k in range(1, STAGES):
-            load(k)
-        nc.sync.dma_start(out=w_sb[:, 1, :].bitcast(I32), in_=words_v[:, 1, :])
-
-        def views(k, lo, hi):
-            dst = grouped[k][:, lo:hi, :].rearrange("p (a i) j -> p a j i", i=4)
-            src = raw[k][:, :, lo:hi].rearrange("p j (a i) -> p a j i", i=4)
-            return dst, src
-
-        def interleave(k):
-            for lo, hi in ((0, PIECE), (PIECE, VEC_COLS[k])):
-                dst, src = views(k, lo, hi)
-                nc.vector.tensor_copy(out=dst, in_=src)
-            dst, src = views(k, VEC_COLS[k], HALF)
-            nc.scalar.copy(out=dst, in_=src)
-
-        def quantize(k):
-            for lo in range(0, HALF, PIECE):
-                cols = slice((k + 1) * HALF + lo, (k + 1) * HALF + lo + PIECE)
-                nc.vector.quantize_mx(
-                    out=codes[:, cols].bitcast(FP8X4),
-                    scales=scales[:, cols],
-                    in_=grouped[k][:, lo : lo + PIECE, :].rearrange("p n j -> p (n j)"),
-                )
-
-        def multiply(k, e):
-            s = k // 2
-            window = slice(k * HALF, k * HALF + N)
-            for c in range(2):
-                rows = slice(c * ROWS, (c + 1) * ROWS)
-                nc.tensor.matmul_mx(
-                    out=acc[k % 2, e, c][:],
-                    lhsT=w_sb[rows, s, 2 * P * e : 2 * P * (e + 1)].bitcast(FP4X4),
-                    lhsT_scale=ws_sb[rows, s, P * e : P * (e + 1)],
-                    rhs=codes[rows, window].bitcast(FP8X4),
-                    rhs_scale=scales[rows, window],
-                    start=True,
-                    stop=True,
-                )
-
-        def finish(k, e):
-            nc.scalar.activation(out=res[k, e][:, 0, :], in_=acc[k % 2, e, 0][:, HALF:N], func=RELU)
-            nc.vector.tensor_scalar_max(out=res[k, e][:, 1, :], in0=acc[k % 2, e, 1][:, HALF:N], scalar1=0.0)
-            nc.sync.dma_start(out=out_v[k // 2, k % 2, e], in_=res[k, e][:])
-
-        def finish_on_scalar(k, e):
-            for c in range(2):
-                nc.scalar.activation(out=res[k, e][:, c, :], in_=acc[k % 2, e, c][:, HALF:N], func=RELU)
-                nc.sync.dma_start(out=out_v[k // 2, k % 2, e][:, c, :], in_=res[k, e][:, c, :])
-
-        for k in range(STAGES):
-            interleave(k)
-            if k == 1:
-                finish_on_scalar(0, 0)
-            if k >= 2:
-                finish_on_scalar(k - 2, 1)
-            quantize(k)
-            multiply(k, 0)
-            multiply(k, 1)
-            if k >= 2:
-                finish(k - 1, 0)
-        finish(STAGES - 2, 1)
-        finish(STAGES - 1, 0)
-        finish(STAGES - 1, 1)
+        nc.vector.memset(codes[:, 0:PAD], 0)
+        nc.vector.memset(scales[:, 0:PAD].bitcast(I32), 0)
+        load(0, 0, 256)
+        load_scales()
+        load_words(0, 1)
+        load(0, 256, 512)
+        load(1, 0, 256)
+        load(1, 256, 512)
+        load_words(1, 2)
+        result(0, 0, 256)
+        result(0, 256, 512)
+        result(1, 0, 256)
+        result(1, 256, 512)
+        interleave(True, 0, 0, 128)
+        interleave(True, 0, 128, 160)
+        interleave(False, 0, 160, 256)
+        quantize(0, 0, 128)
+        quantize(0, 128, 256)
+        multiply(0, 0, 256, (0, 1))
+        interleave(True, 0, 256, 384)
+        interleave(True, 0, 384, 416)
+        interleave(False, 0, 416, 512)
+        quantize(0, 256, 384)
+        quantize(0, 384, 512)
+        multiply(1, 0, 512, (0, 1))
+        relu(False, 0, 0, 0, 0, 0, 256)
+        store(0, 0, 0, 0)
+        relu(False, 0, 0, 1, 0, 0, 256)
+        store(0, 0, 0, 1)
+        relu(False, 0, 1, 0, 0, 0, 256)
+        store(0, 0, 1, 0)
+        relu(False, 0, 1, 1, 0, 0, 256)
+        store(0, 0, 1, 1)
+        interleave(True, 1, 0, 128)
+        interleave(True, 1, 128, 256)
+        quantize(1, 0, 128)
+        quantize(1, 128, 256)
+        multiply(0, 1, 256, (0, 1))
+        relu(False, 1, 0, 0, 0, 256, 512)
+        store(0, 256, 0, 0)
+        relu(False, 1, 0, 1, 0, 256, 512)
+        store(0, 256, 0, 1)
+        interleave(True, 1, 256, 384)
+        interleave(True, 1, 384, 512)
+        relu(False, 1, 1, 0, 0, 256, 512)
+        store(0, 256, 1, 0)
+        relu(False, 1, 1, 1, 0, 256, 512)
+        store(0, 256, 1, 1)
+        quantize(1, 256, 384)
+        quantize(1, 384, 512)
+        multiply(1, 1, 512, (0, 1))
+        relu(False, 0, 0, 0, 1, 0, 256)
+        store(1, 0, 0, 0)
+        relu(True, 0, 0, 1, 1, 0, 256)
+        store(1, 0, 0, 1)
+        relu(False, 0, 1, 0, 1, 0, 256)
+        relu(True, 0, 1, 1, 1, 0, 256)
+        store(1, 0, 1, None)
+        relu(False, 1, 0, 0, 1, 256, 512)
+        relu(True, 1, 0, 1, 1, 256, 512)
+        store(1, 256, 0, None)
+        relu(False, 1, 1, 0, 1, 256, 512)
+        relu(True, 1, 1, 1, 1, 256, 512)
+        store(1, 256, 1, None)

@@ -18,18 +18,16 @@ P = 128
 PACK = 4
 ROWS = 64
 SETS = 2
-HALF = 256
-STAGES = 4
-PIECE = 128
 ALIGN = 256
-PAD = 256
+PAD = 320
+
 
 def tile_rows_glin_relu_kernel(tc, x, w_words, w_scales, out):
     nc = tc.nc
     x_v = x.rearrange("(s c) (p j) n -> s (c p) j n", c=2, j=PACK)
     words_v = w_words.bitcast(I32).rearrange("(s c) p b -> (c p) s b", c=2)
     scales_v = w_scales.bitcast(I32).rearrange("(s c) (q r) b -> r (c q) s b", c=2, r=4)
-    out_v = out.rearrange("(s c) (e p) n -> s p c e n", c=2, p=P)
+    out_v = out.rearrange("(s c) (e p) n -> s e p c n", c=2, p=P)
 
     with ExitStack() as ctx:
         sb = ctx.enter_context(tc.tile_pool(name="sb", bufs=1))
@@ -41,10 +39,9 @@ def tile_rows_glin_relu_kernel(tc, x, w_words, w_scales, out):
         codes = sb.tile([P, PAD + SETS * N], U32, name="codes", align_bytes=ALIGN)
         scales = sb.tile([P, PAD + SETS * N], U8, name="scales", align_bytes=ALIGN)
         acc = {}
-        for b in range(2):
-            for e in range(2):
-                for c in range(2):
-                    acc[b, e, c] = ps.tile([P, N], F32, name="acc%d%d%d" % (b, e, c))
+        for k in range(4):
+            for c in range(2):
+                acc[k, c] = ps.tile([P, N], F32, name="acc%d%d" % (k, c))
         raw = {}
         grouped = {}
         res = {}
@@ -59,15 +56,16 @@ def tile_rows_glin_relu_kernel(tc, x, w_words, w_scales, out):
             grouped[s, lo] = sb.tile([P, hi - lo, PACK], BF16, name="grouped%d_%d" % (s, lo), align_bytes=ALIGN)
             nc.sync.dma_start(out=raw[s, lo][:], in_=x_v[s][:, :, lo:hi])
 
-        def result(s, lo, hi):
-            res[s, lo] = sb.tile([P, 2, 2, hi - lo], F32, name="res%d_%d" % (s, lo), align_bytes=ALIGN)
-
         def load_scales():
             for r in range(4):
                 nc.sync.dma_start(out=ws_sb[r:P:32, :, :].bitcast(I32), in_=scales_v[r])
 
         def load_words(lo, hi):
             nc.sync.dma_start(out=w_sb[:, lo:hi, :].bitcast(I32), in_=words_v[:, lo:hi, :])
+
+        def load_half(s, e):
+            cols = slice(2 * P * e, 2 * P * (e + 1))
+            nc.sync.dma_start(out=w_sb[:, s, cols].bitcast(I32), in_=words_v[:, s, P // 2 * e : P // 2 * (e + 1)])
 
         def interleave(on_vector, s, lo, hi):
             t, base = find(raw, s, lo)
@@ -87,103 +85,110 @@ def tile_rows_glin_relu_kernel(tc, x, w_words, w_scales, out):
                 in_=t[:, lo - base : hi - base, :].rearrange("p n j -> p (n j)"),
             )
 
-        def multiply(b, s, hi, halves):
+        def mul(k, s, e, hi):
             window = slice(PAD + s * N + hi - N, PAD + s * N + hi)
-            for e in halves:
-                ends[b, e] = hi
-                for c in range(2):
-                    rows = slice(c * ROWS, (c + 1) * ROWS)
-                    nc.tensor.matmul_mx(
-                        out=acc[b, e, c][:],
-                        lhsT=w_sb[rows, s, 2 * P * e : 2 * P * (e + 1)].bitcast(FP4X4),
-                        lhsT_scale=ws_sb[rows, s, P * e : P * (e + 1)],
-                        rhs=codes[rows, window].bitcast(FP8X4),
-                        rhs_scale=scales[rows, window],
-                        start=True,
-                        stop=True,
-                    )
+            ends[k] = hi
+            for c in range(2):
+                rows = slice(c * ROWS, (c + 1) * ROWS)
+                nc.tensor.matmul_mx(
+                    out=acc[k, c][:],
+                    lhsT=w_sb[rows, s, 2 * P * e : 2 * P * (e + 1)].bitcast(FP4X4),
+                    lhsT_scale=ws_sb[rows, s, P * e : P * (e + 1)],
+                    rhs=codes[rows, window].bitcast(FP8X4),
+                    rhs_scale=scales[rows, window],
+                    start=True,
+                    stop=True,
+                )
 
-        def relu(on_vector, b, e, c, s, lo, hi):
-            t, base = find(res, s, lo)
-            dst = t[:, c, e, lo - base : hi - base]
-            src = acc[b, e, c][:, N - ends[b, e] + lo : N - ends[b, e] + hi]
+        def empty(on_vector, k, c, s, e, lo, hi):
+            if (s, e, lo) not in res:
+                res[s, e, lo] = sb.tile([P, 2, hi - lo], F32, name="res%d_%d_%d" % (s, e, lo), align_bytes=ALIGN)
+            dst = res[s, e, lo][:, c, :]
+            src = acc[k, c][:, N - ends[k] + lo : N - ends[k] + hi]
             if on_vector:
                 nc.vector.tensor_scalar_max(out=dst, in0=src, scalar1=0.0)
             else:
                 nc.scalar.activation(out=dst, in_=src, func=RELU)
 
-        def store(s, lo, e, c):
-            t = res[s, lo]
-            hi = lo + t.shape[3]
-            if e is None:
-                nc.sync.dma_start(out=out_v[s][:, :, :, lo:hi], in_=t[:])
-            elif c is None:
-                nc.sync.dma_start(out=out_v[s][:, :, e, lo:hi], in_=t[:, :, e, :])
+        def put(s, e, c, lo, hi):
+            t = res[s, e, lo]
+            if c is None:
+                nc.sync.dma_start(out=out_v[s, e][:, :, lo:hi], in_=t[:])
             else:
-                nc.sync.dma_start(out=out_v[s][:, c, e, lo:hi], in_=t[:, c, e, :])
+                nc.sync.dma_start(out=out_v[s, e][:, c, lo:hi], in_=t[:, c, :])
 
         nc.vector.memset(ws_sb[:].bitcast(I32), 0)
         nc.vector.memset(codes[:, 0:PAD], 0)
         nc.vector.memset(scales[:, 0:PAD].bitcast(I32), 0)
-        load(0, 0, 256)
+        load(0, 0, 192)
         load_scales()
         load_words(0, 1)
-        load(0, 256, 512)
-        load(1, 0, 256)
-        load(1, 256, 512)
-        load_words(1, 2)
-        result(0, 0, 256)
-        result(0, 256, 512)
-        result(1, 0, 256)
-        result(1, 256, 512)
-        interleave(True, 0, 0, 128)
-        interleave(True, 0, 128, 160)
-        interleave(False, 0, 160, 256)
-        quantize(0, 0, 128)
-        quantize(0, 128, 256)
-        multiply(0, 0, 256, (0, 1))
-        interleave(True, 0, 256, 384)
-        interleave(True, 0, 384, 416)
-        interleave(False, 0, 416, 512)
-        quantize(0, 256, 384)
+        load(0, 192, 320)
+        load(0, 320, 512)
+        load(1, 0, 192)
+        load_half(1, 0)
+        load(1, 192, 320)
+        load(1, 320, 512)
+        load_half(1, 1)
+        interleave(True, 0, 0, 64)
+        interleave(False, 0, 144, 192)
+        interleave(True, 0, 64, 144)
+        quantize(0, 0, 64)
+        quantize(0, 64, 192)
+        mul(0, 0, 0, 192)
+        interleave(True, 0, 192, 256)
+        interleave(False, 0, 288, 320)
+        interleave(True, 0, 256, 288)
+        quantize(0, 192, 256)
+        quantize(0, 256, 320)
+        mul(1, 0, 1, 320)
+        interleave(True, 0, 320, 384)
+        interleave(False, 0, 464, 512)
+        interleave(True, 0, 384, 464)
+        quantize(0, 320, 384)
         quantize(0, 384, 512)
-        multiply(1, 0, 512, (0, 1))
-        relu(False, 0, 0, 0, 0, 0, 256)
-        store(0, 0, 0, 0)
-        relu(False, 0, 0, 1, 0, 0, 256)
-        store(0, 0, 0, 1)
-        relu(False, 0, 1, 0, 0, 0, 256)
-        store(0, 0, 1, 0)
-        relu(False, 0, 1, 1, 0, 0, 256)
-        store(0, 0, 1, 1)
+        mul(2, 0, 0, 512)
+        mul(3, 0, 1, 512)
+        empty(False, 0, 0, 0, 0, 0, 192)
+        empty(False, 0, 1, 0, 0, 0, 192)
+        put(0, 0, None, 0, 192)
+        empty(False, 1, 0, 0, 1, 0, 320)
+        put(0, 1, 0, 0, 320)
+        empty(False, 1, 1, 0, 1, 0, 320)
+        put(0, 1, 1, 0, 320)
         interleave(True, 1, 0, 128)
-        interleave(True, 1, 128, 256)
+        interleave(True, 1, 128, 192)
         quantize(1, 0, 128)
-        quantize(1, 128, 256)
-        multiply(0, 1, 256, (0, 1))
-        relu(False, 1, 0, 0, 0, 256, 512)
-        store(0, 256, 0, 0)
-        relu(False, 1, 0, 1, 0, 256, 512)
-        store(0, 256, 0, 1)
-        interleave(True, 1, 256, 384)
-        interleave(True, 1, 384, 512)
-        relu(False, 1, 1, 0, 0, 256, 512)
-        store(0, 256, 1, 0)
-        relu(False, 1, 1, 1, 0, 256, 512)
-        store(0, 256, 1, 1)
-        quantize(1, 256, 384)
-        quantize(1, 384, 512)
-        multiply(1, 1, 512, (0, 1))
-        relu(False, 0, 0, 0, 1, 0, 256)
-        store(1, 0, 0, 0)
-        relu(True, 0, 0, 1, 1, 0, 256)
-        store(1, 0, 0, 1)
-        relu(False, 0, 1, 0, 1, 0, 256)
-        relu(True, 0, 1, 1, 1, 0, 256)
-        store(1, 0, 1, None)
-        relu(False, 1, 0, 0, 1, 256, 512)
-        relu(True, 1, 0, 1, 1, 256, 512)
-        store(1, 256, 0, None)
-        relu(False, 1, 1, 0, 1, 256, 512)
-        relu(True, 1, 1, 1, 1, 256, 512)
-        store(1, 256, 1, None)
+        quantize(1, 128, 192)
+        mul(0, 1, 0, 192)
+        interleave(True, 1, 192, 256)
+        interleave(True, 1, 256, 320)
+        quantize(1, 192, 256)
+        quantize(1, 256, 320)
+        mul(1, 1, 1, 320)
+        empty(False, 2, 0, 0, 0, 192, 512)
+        put(0, 0, 0, 192, 512)
+        empty(False, 2, 1, 0, 0, 192, 512)
+        put(0, 0, 1, 192, 512)
+        empty(False, 3, 0, 0, 1, 320, 512)
+        empty(False, 3, 1, 0, 1, 320, 512)
+        put(0, 1, None, 320, 512)
+        interleave(True, 1, 320, 448)
+        interleave(True, 1, 448, 512)
+        quantize(1, 320, 448)
+        quantize(1, 448, 512)
+        mul(2, 1, 0, 512)
+        mul(3, 1, 1, 512)
+        empty(False, 0, 0, 1, 0, 0, 192)
+        empty(True, 0, 1, 1, 0, 0, 192)
+        put(1, 0, None, 0, 192)
+        empty(False, 1, 0, 1, 1, 0, 320)
+        empty(True, 1, 1, 1, 1, 0, 320)
+        put(1, 1, None, 0, 320)
+        empty(False, 2, 0, 1, 0, 192, 512)
+        put(1, 0, 0, 192, 512)
+        empty(True, 2, 1, 1, 0, 192, 512)
+        put(1, 0, 1, 192, 512)
+        empty(False, 3, 0, 1, 1, 320, 512)
+        empty(True, 3, 1, 1, 1, 320, 512)
+        put(1, 1, None, 320, 512)

@@ -19,7 +19,7 @@ PACK = 4
 ROWS = 64
 SETS = 2
 ALIGN = 256
-PAD = 320
+PAD = 256
 
 
 def tile_rows_glin_relu_kernel(tc, x, w_words, w_scales, out):
@@ -120,75 +120,72 @@ def tile_rows_glin_relu_kernel(tc, x, w_words, w_scales, out):
         nc.vector.memset(ws_sb[:].bitcast(I32), 0)
         nc.vector.memset(codes[:, 0:PAD], 0)
         nc.vector.memset(scales[:, 0:PAD].bitcast(I32), 0)
-        load(0, 0, 192)
+        load(0, 0, 256)
         load_scales()
         load_words(0, 1)
-        load(0, 192, 320)
-        load(0, 320, 512)
-        load(1, 0, 192)
+        load(0, 256, 384)
+        load(0, 384, 512)
+        load(1, 0, 128)
+        load(1, 128, 256)
+        load(1, 256, 384)
         load_half(1, 0)
-        load(1, 192, 320)
-        load(1, 320, 512)
+        load(1, 384, 512)
         load_half(1, 1)
-        interleave(True, 0, 0, 64)
-        interleave(False, 0, 144, 192)
-        interleave(True, 0, 64, 144)
-        quantize(0, 0, 64)
-        quantize(0, 64, 192)
-        mul(0, 0, 0, 192)
-        interleave(True, 0, 192, 256)
-        interleave(False, 0, 288, 320)
-        interleave(True, 0, 256, 288)
-        quantize(0, 192, 256)
-        quantize(0, 256, 320)
-        mul(1, 0, 1, 320)
-        interleave(True, 0, 320, 384)
-        interleave(False, 0, 464, 512)
-        interleave(True, 0, 384, 464)
-        quantize(0, 320, 384)
-        quantize(0, 384, 512)
+        interleave(True, 0, 0, 128)
+        interleave(True, 0, 128, 160)
+        interleave(False, 0, 160, 256)
+        quantize(0, 0, 128)
+        quantize(0, 128, 256)
+        mul(0, 0, 0, 256)
+        mul(1, 0, 1, 256)
+        interleave(True, 0, 256, 384)
+        interleave(True, 0, 384, 448)
+        interleave(False, 0, 480, 512)
+        interleave(True, 0, 448, 480)
+        quantize(0, 256, 384)
+        quantize(0, 384, 448)
+        quantize(0, 448, 512)
         mul(2, 0, 0, 512)
         mul(3, 0, 1, 512)
-        empty(False, 0, 0, 0, 0, 0, 192)
-        empty(False, 0, 1, 0, 0, 0, 192)
-        put(0, 0, None, 0, 192)
-        empty(False, 1, 0, 0, 1, 0, 320)
-        put(0, 1, 0, 0, 320)
-        empty(False, 1, 1, 0, 1, 0, 320)
-        put(0, 1, 1, 0, 320)
+        empty(False, 0, 0, 0, 0, 0, 256)
+        put(0, 0, 0, 0, 256)
+        empty(False, 0, 1, 0, 0, 0, 256)
+        put(0, 0, 1, 0, 256)
+        empty(False, 1, 0, 0, 1, 0, 256)
+        empty(False, 1, 1, 0, 1, 0, 256)
+        put(0, 1, None, 0, 256)
         interleave(True, 1, 0, 128)
         interleave(True, 1, 128, 192)
+        interleave(True, 1, 192, 256)
         quantize(1, 0, 128)
         quantize(1, 128, 192)
-        mul(0, 1, 0, 192)
-        interleave(True, 1, 192, 256)
-        interleave(True, 1, 256, 320)
         quantize(1, 192, 256)
-        quantize(1, 256, 320)
-        mul(1, 1, 1, 320)
-        empty(False, 2, 0, 0, 0, 192, 512)
-        put(0, 0, 0, 192, 512)
-        empty(False, 2, 1, 0, 0, 192, 512)
-        put(0, 0, 1, 192, 512)
-        empty(False, 3, 0, 0, 1, 320, 512)
-        empty(False, 3, 1, 0, 1, 320, 512)
-        put(0, 1, None, 320, 512)
-        interleave(True, 1, 320, 448)
+        mul(0, 1, 0, 256)
+        mul(1, 1, 1, 256)
+        empty(False, 2, 0, 0, 0, 256, 512)
+        put(0, 0, 0, 256, 512)
+        empty(False, 2, 1, 0, 0, 256, 512)
+        put(0, 0, 1, 256, 512)
+        empty(False, 3, 0, 0, 1, 256, 512)
+        empty(False, 3, 1, 0, 1, 256, 512)
+        put(0, 1, None, 256, 512)
+        interleave(True, 1, 256, 384)
+        interleave(True, 1, 384, 448)
         interleave(True, 1, 448, 512)
-        quantize(1, 320, 448)
+        quantize(1, 256, 384)
+        quantize(1, 384, 448)
         quantize(1, 448, 512)
         mul(2, 1, 0, 512)
         mul(3, 1, 1, 512)
-        empty(False, 0, 0, 1, 0, 0, 192)
-        empty(True, 0, 1, 1, 0, 0, 192)
-        put(1, 0, None, 0, 192)
-        empty(False, 1, 0, 1, 1, 0, 320)
-        empty(True, 1, 1, 1, 1, 0, 320)
-        put(1, 1, None, 0, 320)
-        empty(False, 2, 0, 1, 0, 192, 512)
-        put(1, 0, 0, 192, 512)
-        empty(True, 2, 1, 1, 0, 192, 512)
-        put(1, 0, 1, 192, 512)
-        empty(False, 3, 0, 1, 1, 320, 512)
-        empty(True, 3, 1, 1, 1, 320, 512)
-        put(1, 1, None, 320, 512)
+        empty(False, 0, 0, 1, 0, 0, 256)
+        empty(True, 0, 1, 1, 0, 0, 256)
+        put(1, 0, None, 0, 256)
+        empty(False, 1, 0, 1, 1, 0, 256)
+        empty(True, 1, 1, 1, 1, 0, 256)
+        put(1, 1, None, 0, 256)
+        empty(False, 2, 0, 1, 0, 256, 512)
+        empty(True, 2, 1, 1, 0, 256, 512)
+        put(1, 0, None, 256, 512)
+        empty(False, 3, 0, 1, 1, 256, 512)
+        empty(True, 3, 1, 1, 1, 256, 512)
+        put(1, 1, None, 256, 512)

@@ -123,37 +123,35 @@ def tile_rows_glin_relu_kernel(tc, x, w_words, w_scales, out):
         load(0, 0, 256)
         load_scales()
         load_words(0, 1)
-        load(0, 256, 384)
-        load(0, 384, 512)
-        load(1, 0, 128)
-        load(1, 128, 256)
-        load(1, 256, 384)
+        load(0, 256, 512)
+        load(1, 0, 256)
+        load(1, 256, 512)
         load_half(1, 0)
-        load(1, 384, 512)
         load_half(1, 1)
         interleave(True, 0, 0, 128)
-        interleave(True, 0, 128, 160)
-        interleave(False, 0, 160, 256)
+        interleave(False, 0, 192, 256)
+        interleave(True, 0, 128, 192)
         quantize(0, 0, 128)
-        quantize(0, 128, 256)
+        quantize(0, 192, 256)
+        quantize(0, 128, 192)
         mul(0, 0, 0, 256)
         mul(1, 0, 1, 256)
         interleave(True, 0, 256, 384)
+        interleave(False, 0, 448, 512)
         interleave(True, 0, 384, 448)
-        interleave(False, 0, 480, 512)
-        interleave(True, 0, 448, 480)
         quantize(0, 256, 384)
-        quantize(0, 384, 448)
         quantize(0, 448, 512)
-        mul(2, 0, 0, 512)
-        mul(3, 0, 1, 512)
+        quantize(0, 384, 448)
+        mul(2, 0, 1, 512)
+        mul(3, 0, 0, 512)
         empty(False, 0, 0, 0, 0, 0, 256)
         put(0, 0, 0, 0, 256)
         empty(False, 0, 1, 0, 0, 0, 256)
         put(0, 0, 1, 0, 256)
         empty(False, 1, 0, 0, 1, 0, 256)
+        put(0, 1, 0, 0, 256)
         empty(False, 1, 1, 0, 1, 0, 256)
-        put(0, 1, None, 0, 256)
+        put(0, 1, 1, 0, 256)
         interleave(True, 1, 0, 128)
         interleave(True, 1, 128, 192)
         interleave(True, 1, 192, 256)
@@ -162,30 +160,32 @@ def tile_rows_glin_relu_kernel(tc, x, w_words, w_scales, out):
         quantize(1, 192, 256)
         mul(0, 1, 0, 256)
         mul(1, 1, 1, 256)
-        empty(False, 2, 0, 0, 0, 256, 512)
+        empty(False, 2, 0, 0, 1, 256, 512)
+        put(0, 1, 0, 256, 512)
+        empty(False, 2, 1, 0, 1, 256, 512)
+        put(0, 1, 1, 256, 512)
+        empty(False, 3, 0, 0, 0, 256, 512)
         put(0, 0, 0, 256, 512)
-        empty(False, 2, 1, 0, 0, 256, 512)
+        empty(False, 3, 1, 0, 0, 256, 512)
         put(0, 0, 1, 256, 512)
-        empty(False, 3, 0, 0, 1, 256, 512)
-        empty(False, 3, 1, 0, 1, 256, 512)
-        put(0, 1, None, 256, 512)
         interleave(True, 1, 256, 384)
         interleave(True, 1, 384, 448)
         interleave(True, 1, 448, 512)
         quantize(1, 256, 384)
         quantize(1, 384, 448)
         quantize(1, 448, 512)
-        mul(2, 1, 0, 512)
-        mul(3, 1, 1, 512)
+        mul(2, 1, 1, 512)
+        mul(3, 1, 0, 512)
         empty(False, 0, 0, 1, 0, 0, 256)
+        put(1, 0, 0, 0, 256)
         empty(True, 0, 1, 1, 0, 0, 256)
-        put(1, 0, None, 0, 256)
+        put(1, 0, 1, 0, 256)
         empty(False, 1, 0, 1, 1, 0, 256)
         empty(True, 1, 1, 1, 1, 0, 256)
         put(1, 1, None, 0, 256)
-        empty(False, 2, 0, 1, 0, 256, 512)
-        empty(True, 2, 1, 1, 0, 256, 512)
-        put(1, 0, None, 256, 512)
-        empty(False, 3, 0, 1, 1, 256, 512)
-        empty(True, 3, 1, 1, 1, 256, 512)
+        empty(False, 2, 0, 1, 1, 256, 512)
+        empty(True, 2, 1, 1, 1, 256, 512)
         put(1, 1, None, 256, 512)
+        empty(False, 3, 0, 1, 0, 256, 512)
+        empty(True, 3, 1, 1, 0, 256, 512)
+        put(1, 0, None, 256, 512)

@@ -20,6 +20,7 @@ ROWS = 64
 SETS = 2
 ALIGN = 256
 PAD = 256
+BANK = ((0, 1, 2, 0, 3, 2, 1, 0), (0, 1, 2, 0, 3, 1, 2, 0))
 
 
 def tile_rows_glin_relu_kernel(tc, x, w_words, w_scales, out):
@@ -91,7 +92,7 @@ def tile_rows_glin_relu_kernel(tc, x, w_words, w_scales, out):
             for c in range(2):
                 rows = slice(c * ROWS, (c + 1) * ROWS)
                 nc.tensor.matmul_mx(
-                    out=acc[k, c][:],
+                    out=acc[BANK[c][k], c][:],
                     lhsT=w_sb[rows, s, 2 * P * e : 2 * P * (e + 1)].bitcast(FP4X4),
                     lhsT_scale=ws_sb[rows, s, P * e : P * (e + 1)],
                     rhs=codes[rows, window].bitcast(FP8X4),
@@ -104,7 +105,7 @@ def tile_rows_glin_relu_kernel(tc, x, w_words, w_scales, out):
             if (s, e, lo) not in res:
                 res[s, e, lo] = sb.tile([P, 2, hi - lo], F32, name="res%d_%d_%d" % (s, e, lo), align_bytes=ALIGN)
             dst = res[s, e, lo][:, c, :]
-            src = acc[k, c][:, N - ends[k] + lo : N - ends[k] + hi]
+            src = acc[BANK[c][k], c][:, N - ends[k] + lo : N - ends[k] + hi]
             if on_vector:
                 nc.vector.tensor_scalar_max(out=dst, in0=src, scalar1=0.0)
             else:
@@ -128,26 +129,30 @@ def tile_rows_glin_relu_kernel(tc, x, w_words, w_scales, out):
         load(1, 256, 512)
         load_half(1, 0)
         load_half(1, 1)
-        interleave(True, 0, 0, 128)
+        interleave(True, 0, 0, 64)
         interleave(False, 0, 192, 256)
+        interleave(True, 0, 64, 128)
         interleave(True, 0, 128, 192)
-        quantize(0, 0, 128)
+        quantize(0, 0, 64)
+        quantize(0, 64, 128)
         quantize(0, 192, 256)
         quantize(0, 128, 192)
         mul(0, 0, 0, 256)
         mul(1, 0, 1, 256)
-        interleave(True, 0, 256, 384)
+        interleave(True, 0, 256, 320)
         interleave(False, 0, 448, 512)
+        interleave(True, 0, 320, 384)
         interleave(True, 0, 384, 448)
-        quantize(0, 256, 384)
+        quantize(0, 256, 320)
+        quantize(0, 320, 384)
         quantize(0, 448, 512)
         quantize(0, 384, 448)
         mul(2, 0, 1, 512)
-        mul(3, 0, 0, 512)
         empty(False, 0, 0, 0, 0, 0, 256)
         put(0, 0, 0, 0, 256)
         empty(False, 0, 1, 0, 0, 0, 256)
         put(0, 0, 1, 0, 256)
+        mul(3, 0, 0, 512)
         empty(False, 1, 0, 0, 1, 0, 256)
         put(0, 1, 0, 0, 256)
         empty(False, 1, 1, 0, 1, 0, 256)
@@ -158,10 +163,10 @@ def tile_rows_glin_relu_kernel(tc, x, w_words, w_scales, out):
         quantize(1, 0, 128)
         quantize(1, 128, 192)
         quantize(1, 192, 256)
-        mul(0, 1, 0, 256)
-        mul(1, 1, 1, 256)
+        mul(4, 1, 0, 256)
         empty(False, 2, 0, 0, 1, 256, 512)
         put(0, 1, 0, 256, 512)
+        mul(5, 1, 1, 256)
         empty(False, 2, 1, 0, 1, 256, 512)
         put(0, 1, 1, 256, 512)
         empty(False, 3, 0, 0, 0, 256, 512)
@@ -174,18 +179,18 @@ def tile_rows_glin_relu_kernel(tc, x, w_words, w_scales, out):
         quantize(1, 256, 384)
         quantize(1, 384, 448)
         quantize(1, 448, 512)
-        mul(2, 1, 1, 512)
-        mul(3, 1, 0, 512)
-        empty(False, 0, 0, 1, 0, 0, 256)
+        mul(6, 1, 1, 512)
+        mul(7, 1, 0, 512)
+        empty(False, 4, 0, 1, 0, 0, 256)
         put(1, 0, 0, 0, 256)
-        empty(True, 0, 1, 1, 0, 0, 256)
+        empty(True, 4, 1, 1, 0, 0, 256)
         put(1, 0, 1, 0, 256)
-        empty(False, 1, 0, 1, 1, 0, 256)
-        empty(True, 1, 1, 1, 1, 0, 256)
+        empty(True, 5, 0, 1, 1, 0, 256)
+        empty(False, 5, 1, 1, 1, 0, 256)
         put(1, 1, None, 0, 256)
-        empty(False, 2, 0, 1, 1, 256, 512)
-        empty(True, 2, 1, 1, 1, 256, 512)
+        empty(True, 6, 0, 1, 1, 256, 512)
+        empty(False, 6, 1, 1, 1, 256, 512)
         put(1, 1, None, 256, 512)
-        empty(False, 3, 0, 1, 0, 256, 512)
-        empty(True, 3, 1, 1, 0, 256, 512)
+        empty(True, 7, 0, 1, 0, 256, 512)
+        empty(False, 7, 1, 1, 0, 256, 512)
         put(1, 0, None, 256, 512)

@@ -20,6 +20,7 @@ ROWS = 64
 SETS = 2
 ALIGN = 256
 PAD = 256
+SHIFT = 128
 BANK = ((0, 1, 2, 0, 3, 2, 1, 0), (0, 1, 2, 0, 3, 1, 2, 0))
 
 
@@ -38,7 +39,8 @@ def tile_rows_glin_relu_kernel(tc, x, w_words, w_scales, out):
         w_sb = sb.tile([P, SETS, 2 * M], U8, name="w_sb", align_bytes=ALIGN)
         ws_sb = sb.tile([P, SETS, M], U8, name="ws_sb", align_bytes=ALIGN)
         codes = sb.tile([P, PAD + SETS * N], U32, name="codes", align_bytes=ALIGN)
-        scales = sb.tile([P, PAD + SETS * N], U8, name="scales", align_bytes=ALIGN)
+        scales_all = sb.tile([P, SHIFT + PAD + SETS * N], U8, name="scales", align_bytes=ALIGN)
+        scales = scales_all[:, SHIFT:]
         acc = {}
         for k in range(4):
             for c in range(2):

from contextlib import ExitStack

import concourse.mybir as mybir

G, D, M, N = 4, 256, 256, 512
FLOPS = 2 * G * D * M * N

F32 = mybir.dt.float32
BF16 = mybir.dt.bfloat16
I32 = mybir.dt.int32
U32 = mybir.dt.uint32
U8 = mybir.dt.uint8
FP8X4 = mybir.dt.float8_e4m3fn_x4
FP4X4 = mybir.dt.float4_e2m1fn_x4
RELU = mybir.ActivationFunctionType.Relu

P = 128
PACK = 4
ROWS = 64
SETS = 2
ALIGN = 256
PAD = 256
SHIFT = 128
BANK = ((0, 1, 2, 0, 3, 2, 1, 0), (0, 1, 2, 0, 3, 1, 2, 0))


def tile_rows_glin_relu_kernel(tc, x, w_words, w_scales, out):
    nc = tc.nc
    x_v = x.rearrange("(s c) (p j) n -> s (c p) j n", c=2, j=PACK)
    words_v = w_words.bitcast(I32).rearrange("(s c) p b -> (c p) s b", c=2)
    scales_v = w_scales.bitcast(I32).rearrange("(s c) (q r) b -> r (c q) s b", c=2, r=4)
    out_v = out.rearrange("(s c) (e p) n -> s e p c n", c=2, p=P)

    with ExitStack() as ctx:
        sb = ctx.enter_context(tc.tile_pool(name="sb", bufs=1))
        ps = ctx.enter_context(tc.psum_pool(name="ps", bufs=1))
        ctx.enter_context(tc.manual_schedule())

        w_sb = sb.tile([P, SETS, 2 * M], U8, name="w_sb", align_bytes=ALIGN)
        ws_sb = sb.tile([P, SETS, M], U8, name="ws_sb", align_bytes=ALIGN)
        codes = sb.tile([P, PAD + SETS * N], U32, name="codes", align_bytes=ALIGN)
        scales_all = sb.tile([P, SHIFT + PAD + SETS * N], U8, name="scales", align_bytes=ALIGN)
        scales = scales_all[:, SHIFT:]
        acc = {}
        for k in range(4):
            for c in range(2):
                acc[k, c] = ps.tile([P, N], F32, name="acc%d%d" % (k, c))
        raw = {}
        grouped = {}
        res = {}
        ends = {}

        def find(tiles, s, lo):
            base = max(b for (ss, b) in tiles if ss == s and b <= lo)
            return tiles[s, base], base

        def load(s, lo, hi):
            raw[s, lo] = sb.tile([P, PACK, hi - lo], F32, name="raw%d_%d" % (s, lo), align_bytes=ALIGN)
            grouped[s, lo] = sb.tile([P, hi - lo, PACK], BF16, name="grouped%d_%d" % (s, lo), align_bytes=ALIGN)
            nc.sync.dma_start(out=raw[s, lo][:], in_=x_v[s][:, :, lo:hi])

        def load_scales():
            for r in range(4):
                nc.sync.dma_start(out=ws_sb[r:P:32, :, :].bitcast(I32), in_=scales_v[r])

        def load_words(lo, hi):
            nc.sync.dma_start(out=w_sb[:, lo:hi, :].bitcast(I32), in_=words_v[:, lo:hi, :])

        def load_half(s, e):
            cols = slice(2 * P * e, 2 * P * (e + 1))
            nc.sync.dma_start(out=w_sb[:, s, cols].bitcast(I32), in_=words_v[:, s, P // 2 * e : P // 2 * (e + 1)])

        def interleave(on_vector, s, lo, hi):
            t, base = find(raw, s, lo)
            dst = grouped[s, base][:, lo - base : hi - base, :].rearrange("p (a i) j -> p a j i", i=4)
            src = t[:, :, lo - base : hi - base].rearrange("p j (a i) -> p a j i", i=4)
            if on_vector:
                nc.vector.tensor_copy(out=dst, in_=src)
            else:
                nc.scalar.copy(out=dst, in_=src)

        def quantize(s, lo, hi):
            t, base = find(grouped, s, lo)
            cols = slice(PAD + s * N + lo, PAD + s * N + hi)
            nc.vector.quantize_mx(
                out=codes[:, cols].bitcast(FP8X4),
                scales=scales[:, cols],
                in_=t[:, lo - base : hi - base, :].rearrange("p n j -> p (n j)"),
            )

        def mul(k, s, e, hi):
            window = slice(PAD + s * N + hi - N, PAD + s * N + hi)
            ends[k] = hi
            for c in range(2):
                rows = slice(c * ROWS, (c + 1) * ROWS)
                nc.tensor.matmul_mx(
                    out=acc[BANK[c][k], c][:],
                    lhsT=w_sb[rows, s, 2 * P * e : 2 * P * (e + 1)].bitcast(FP4X4),
                    lhsT_scale=ws_sb[rows, s, P * e : P * (e + 1)],
                    rhs=codes[rows, window].bitcast(FP8X4),
                    rhs_scale=scales[rows, window],
                    start=True,
                    stop=True,
                )

        def empty(on_vector, k, c, s, e, lo, hi):
            if (s, e, lo) not in res:
                res[s, e, lo] = sb.tile([P, 2, hi - lo], F32, name="res%d_%d_%d" % (s, e, lo), align_bytes=ALIGN)
            dst = res[s, e, lo][:, c, :]
            src = acc[BANK[c][k], c][:, N - ends[k] + lo : N - ends[k] + hi]
            if on_vector:
                nc.vector.tensor_scalar_max(out=dst, in0=src, scalar1=0.0)
            else:
                nc.scalar.activation(out=dst, in_=src, func=RELU)

        def put(s, e, c, lo, hi):
            t = res[s, e, lo]
            if c is None:
                nc.sync.dma_start(out=out_v[s, e][:, :, lo:hi], in_=t[:])
            else:
                nc.sync.dma_start(out=out_v[s, e][:, c, lo:hi], in_=t[:, c, :])

        nc.vector.memset(ws_sb[:].bitcast(I32), 0)
        nc.vector.memset(codes[:, 0:PAD], 0)
        nc.vector.memset(scales[:, 0:PAD].bitcast(I32), 0)
        load(0, 0, 256)
        load_scales()
        load_words(0, 1)
        load(0, 256, 512)
        load(1, 0, 256)
        load(1, 256, 512)
        load_half(1, 0)
        load_half(1, 1)
        interleave(True, 0, 0, 64)
        interleave(False, 0, 192, 256)
        interleave(True, 0, 64, 128)
        interleave(True, 0, 128, 192)
        quantize(0, 0, 64)
        quantize(0, 64, 128)
        quantize(0, 192, 256)
        quantize(0, 128, 192)
        mul(0, 0, 0, 256)
        mul(1, 0, 1, 256)
        interleave(True, 0, 256, 320)
        interleave(False, 0, 448, 512)
        interleave(True, 0, 320, 384)
        interleave(True, 0, 384, 448)
        quantize(0, 256, 320)
        quantize(0, 320, 384)
        quantize(0, 448, 512)
        quantize(0, 384, 448)
        mul(2, 0, 1, 512)
        empty(False, 0, 0, 0, 0, 0, 256)
        put(0, 0, 0, 0, 256)
        empty(False, 0, 1, 0, 0, 0, 256)
        put(0, 0, 1, 0, 256)
        mul(3, 0, 0, 512)
        empty(False, 1, 0, 0, 1, 0, 256)
        put(0, 1, 0, 0, 256)
        empty(False, 1, 1, 0, 1, 0, 256)
        put(0, 1, 1, 0, 256)
        interleave(True, 1, 0, 128)
        interleave(True, 1, 128, 192)
        interleave(True, 1, 192, 256)
        quantize(1, 0, 128)
        quantize(1, 128, 192)
        quantize(1, 192, 256)
        mul(4, 1, 0, 256)
        empty(False, 2, 0, 0, 1, 256, 512)
        put(0, 1, 0, 256, 512)
        mul(5, 1, 1, 256)
        empty(False, 2, 1, 0, 1, 256, 512)
        put(0, 1, 1, 256, 512)
        empty(False, 3, 0, 0, 0, 256, 512)
        put(0, 0, 0, 256, 512)
        empty(False, 3, 1, 0, 0, 256, 512)
        put(0, 0, 1, 256, 512)
        interleave(True, 1, 256, 384)
        interleave(True, 1, 384, 448)
        interleave(True, 1, 448, 512)
        quantize(1, 256, 384)
        quantize(1, 384, 448)
        quantize(1, 448, 512)
        mul(6, 1, 1, 512)
        mul(7, 1, 0, 512)
        empty(False, 4, 0, 1, 0, 0, 256)
        put(1, 0, 0, 0, 256)
        empty(True, 4, 1, 1, 0, 0, 256)
        put(1, 0, 1, 0, 256)
        empty(True, 5, 0, 1, 1, 0, 256)
        empty(False, 5, 1, 1, 1, 0, 256)
        put(1, 1, None, 0, 256)
        empty(True, 6, 0, 1, 1, 256, 512)
        empty(False, 6, 1, 1, 1, 256, 512)
        put(1, 1, None, 256, 512)
        empty(True, 7, 0, 1, 0, 256, 512)
        empty(False, 7, 1, 1, 0, 256, 512)
        put(1, 0, None, 256, 512)
